import numpy as np
import ml_dtypes


def mxq(x, axis, fmt="e4m3"):
    dtype, down = {"e4m3": (ml_dtypes.float8_e4m3fn, 7), "e5m2": (ml_dtypes.float8_e5m2, 14)}[fmt]
    v = np.moveaxis(np.asarray(x, np.float32).astype(ml_dtypes.bfloat16).astype(np.float64), axis, -1)
    blocks = v.reshape(v.shape[:-1] + (-1, 32))
    amax = np.abs(blocks).max(-1, keepdims=True)
    byte = np.maximum(np.where(amax > 0, np.frexp(amax)[1] - 1 + 127, 0) - down, 1)
    scale = np.exp2(byte - 127.0)
    codes = (blocks / scale).astype(np.float32).astype(dtype).astype(np.float64)
    return np.moveaxis((codes * scale).reshape(v.shape), -1, axis)


WIDE = False


def mx_kscale(k):
    if not WIDE:
        return np.ones(k)
    levels = np.array([10, -10, 5, -5, 0])
    if k % 512:
        return np.exp2(np.random.permutation(np.resize(levels, k // 32))).repeat(32)
    a = np.empty((k // 512, 16))
    for p in range(k // 512):
        a[p, :8] = np.random.permutation(np.resize(levels, 8))
        for g in range(8):
            far = levels[np.abs(levels - a[p, g]) >= 10]
            a[p, g + 8] = far[np.random.randint(len(far))]
    return np.exp2(a.ravel()).repeat(32)


def f64(x):
    return np.asarray(x).astype(np.float64)


def striped(idx):
    return np.tile(idx.reshape(-1, 16).T, (8, 1)).astype(np.uint16)


def unstriped(offs):
    return offs[:16].T.reshape(-1).astype(np.int64)


E2M1 = np.array([0.0, 0.5, 1.0, 1.5, 2.0, 3.0, 4.0, 6.0, -0.0, -0.5, -1.0, -1.5, -2.0, -3.0, -4.0, -6.0])


def pack_weight(w, fmt):
    k, n = w.shape
    w = f64(np.asarray(w, np.float32).astype(ml_dtypes.bfloat16)).reshape(k // 32, 32, n)
    amax = np.abs(w).max(1)
    if fmt == "e4m3":
        byte = np.frexp(amax)[1] - 1 + 127 - 7
    else:
        mant, ex = np.frexp(amax / 6.0)
        byte = np.where(mant > 0.5, ex, ex - 1) + 127
    byte = np.clip(np.where(amax > 0, byte, 1), 1, 254)
    scaled = (w * np.exp2(127.0 - byte)[:, None, :]).reshape(k, n).astype(np.float32)
    by_word = np.ascontiguousarray(scaled.reshape(k // 512, 128, 4, n).transpose(0, 1, 3, 2))
    if fmt == "e4m3":
        words = by_word.astype(ml_dtypes.float8_e4m3fn).view(np.uint8)
    else:
        c = by_word.astype(ml_dtypes.float4_e2m1fn).view(np.uint8) & 0xF
        words = (c[..., 0::2] | (c[..., 1::2] << 4)).reshape(k // 512, 128, 2 * n)
    return np.ascontiguousarray(words), np.ascontiguousarray(byte.astype(np.uint8).reshape(k // 512, 16, n))


def unpack_weight(words, scales, fmt):
    g, _, n = scales.shape
    words = np.ascontiguousarray(words).reshape(g, 128, n, -1)
    if fmt == "e4m3":
        vals = words.view(ml_dtypes.float8_e4m3fn).astype(np.float64)
    else:
        nib = np.empty((g, 128, n, 4), np.uint8)
        nib[..., 0::2] = words & 0xF
        nib[..., 1::2] = words >> 4
        vals = E2M1[nib]
    vals = vals * np.repeat(np.exp2(scales.astype(np.float64) - 127.0), 8, axis=1)[..., None]
    return vals.transpose(0, 1, 3, 2).reshape(g * 512, n)


def gelu(v):
    return 0.5 * v * (1.0 + np.tanh(np.sqrt(2.0 / np.pi) * (v + 0.044715 * v**3)))


def bf(x):
    return np.asarray(x, np.float32).astype(ml_dtypes.bfloat16)


def planes(Y):
    n, m = Y.shape
    b = f64(bf(Y)).reshape(n // 32, 32, m)
    amax = np.abs(b).max(1)
    byte = np.clip(np.where(amax > 0, np.frexp(amax)[1] - 1 + 127 - 7, 1), 1, 254)
    codes = (b * np.exp2(127.0 - byte)[:, None, :]).reshape(n, m).astype(np.float32).astype(ml_dtypes.float8_e4m3fn).view(np.uint8)
    words = codes.reshape(n // 512, 128, 4, m).transpose(0, 1, 3, 2)
    return np.ascontiguousarray(words), np.ascontiguousarray(byte.astype(np.uint8).reshape(n // 512, 16, m))


K, T, S, H, T2, P, N = 1024, 4096, 1024, 512, 2048, 1024, 384

def setup_inputs():
    n = np.random.standard_normal
    s = mx_kscale(K)[:, None]
    u = mx_kscale(H)[:, None]
    d = {}
    d["tab_words"], d["tab_scales"] = pack_weight(n((K, T)) * s, "e4m3")
    d["offs"] = striped(np.random.permutation(T)[:S])
    d["offs2"] = striped(np.random.permutation(T2)[:S])
    d["offs3"] = striped(np.random.permutation(T2)[:P])
    d["w1"] = (1.8 * n((K, H)) / K ** 0.5 / s).astype(np.float32)
    d["w2_words"], d["w2_scales"] = pack_weight(0.8 * n((K, H)) / K ** 0.5 / s, "e2m1")
    d["w3"] = (0.8 * n((K, H)) / K ** 0.5 / s).astype(np.float32)
    d["gain"] = (np.exp(0.3 * n(H)) * u[:, 0]).astype(np.float32)
    d["wgs"] = np.exp(0.3 * n((128, S))).astype(np.float32)
    d["page0"] = (n((H, T2)) * u).astype(np.float32)
    d["bias"] = (0.8 * n(H) * u[:, 0]).astype(np.float32)
    d["w4_words"], d["w4_scales"] = pack_weight(0.7 * n((H, N)) / H ** 0.5 / u, "e4m3")
    return d

def reference(tab_words, tab_scales, offs, offs2, offs3, w1, w2_words, w2_scales, w3, gain, wgs, page0, bias, w4_words, w4_scales):
    v = unpack_weight(tab_words, tab_scales, "e4m3")[:, unstriped(offs)]
    w2 = unpack_weight(w2_words, w2_scales, "e2m1")
    w4 = unpack_weight(w4_words, w4_scales, "e4m3")
    a = np.tanh(mxq(f64(w1), 0, "e4m3").T @ v)
    b = np.abs((w2.T @ v) + a)
    h = f64(gain)[:, None] * ((mxq(f64(w3), 0, "e4m3").T @ v) + b)
    page = f64(page0).copy()
    page[:, unstriped(offs2)] = np.tile(f64(wgs), (H // 128, 1)) * h
    x = page[:, unstriped(offs3)] + f64(bias)[:, None]
    y = np.square(w4.T @ mxq(x, 0, "e4m3"))
    words, scales = planes(page)
    return y, page, words, scales

@@ -1,0 +1,222 @@
+from contextlib import ExitStack
+
+import concourse.mybir as mybir
+
+K, T, S, H, T2, NP, N = 1024, 4096, 1024, 512, 2048, 1024, 384
+FLOPS = 2 * (3 * K * H * S + H * N * NP)
+
+F32 = mybir.dt.float32
+BF16 = mybir.dt.bfloat16
+I32 = mybir.dt.int32
+U32 = mybir.dt.uint32
+U16 = mybir.dt.uint16
+U8 = mybir.dt.uint8
+FP8X4 = mybir.dt.float8_e4m3fn_x4
+FP4X4 = mybir.dt.float4_e2m1fn_x4
+ACT = mybir.ActivationFunctionType
+ALU = mybir.AluOpType
+
+P = 128
+PACK = 4
+HALF = 512
+LCOLS = HALF // 16
+
+
+def cols(i, width):
+    return slice(i * width, (i + 1) * width)
+
+
+def tile_list_capsule_segment_scores_kernel(
+    tc, tab_words, tab_scales, offs, offs2, offs3, w1, w2_words, w2_scales, w3, gain, wgs, page0, bias,
+    w4_words, w4_scales, out_0, out_1, out_2, out_3,
+):
+    nc = tc.nc
+    with ExitStack() as ctx:
+        keep = ctx.enter_context(tc.tile_pool(name="keep", bufs=1))
+        ring = ctx.enter_context(tc.tile_pool(name="ring", bufs=2))
+        psum = ctx.enter_context(tc.psum_pool(name="psum", bufs=2))
+
+        def held(shape, dtype, name):
+            return keep.tile(shape, dtype, name=name, align_bytes=64)
+
+        list1 = held([P, S // 16], U16, "list1")
+        list2 = held([P, S // 16], U16, "list2")
+        list3 = held([P, NP // 16], U16, "list3")
+
+        tab_sc = held([P, T], U8, "tab_sc")
+        w2_sc_raw = held([P, 2, H], U8, "w2_sc_raw")
+        v_sc1 = held([P, S], U8, "v_sc1")
+        w4_sc = held([P, N], U8, "w4_sc")
+        for plane in (tab_sc[:], w2_sc_raw[:].rearrange("p a c -> p (a c)"), v_sc1[:], w4_sc[:]):
+            nc.vector.memset(plane.bitcast(I32), 0)
+
+        def load_weight(w, a, name):
+            raw = held([P, PACK, H], F32, name)
+            nc.sync.dma_start(raw[:], w[512 * a : 512 * (a + 1), :].rearrange("(p j) c -> p j c", j=PACK))
+            return raw
+
+        def load_table(a):
+            words = held([P, T], U32, "tab%d" % a)
+            nc.sync.dma_start(words[:].bitcast(I32), tab_words[a].rearrange("p t i -> p (t i)").bitcast(I32))
+            return words
+
+        nc.sync.dma_start(list1[:], offs)
+        tab = [load_table(0)]
+        for q in range(4):
+            nc.scalar.dma_start(tab_sc[32 * q : 32 * q + 8, :].bitcast(I32), tab_scales[:, 4 * q : 4 * q + 4, :].bitcast(I32))
+        w2_raw = held([P, 2, 2 * H], U8, "w2_raw")
+        nc.sync.dma_start(w2_raw[:].bitcast(I32), w2_words.rearrange("a p n -> p a n").bitcast(I32))
+        tab.append(load_table(1))
+        for q in range(4):
+            nc.scalar.dma_start(
+                w2_sc_raw[32 * q : 32 * q + 4, :, :].bitcast(I32),
+                w2_scales[:, 4 * q : 4 * q + 4, :].rearrange("a r c -> r a c").bitcast(I32),
+            )
+        w1_raw = [load_weight(w1, a, "w1_raw%d" % a) for a in range(2)]
+        w3_raw = [load_weight(w3, a, "w3_raw%d" % a) for a in range(2)]
+        gain_sb = held([P, PACK], F32, "gain_sb")
+        nc.gpsimd.dma_start(gain_sb[:], gain.rearrange("(p t) -> p t", t=PACK))
+        bias_sb = held([P, PACK], F32, "bias_sb")
+        nc.gpsimd.dma_start(bias_sb[:], bias.rearrange("(p t) -> p t", t=PACK))
+        wgs_rows = wgs.rearrange("(i t) j -> i t j", t=PACK)
+        wg_first = held([P, 1, S], F32, "wg_first")
+        wg_rest = held([P, 3, S], F32, "wg_rest")
+        page_rows = page0.rearrange("(p t) m -> p t m", t=PACK)
+        page = [held([P, T2], F32, "page%d" % t) for t in range(PACK)]
+        for q in range(4):
+            nc.sync.dma_start(wg_first[32 * q : 32 * q + 32, :, :], wgs_rows[:, 0:1, :])
+        nc.sync.dma_start(list2[:], offs2)
+        nc.sync.dma_start(page[0][:], page_rows[:, 0, :])
+        for q in range(4):
+            nc.sync.dma_start(wg_rest[32 * q : 32 * q + 32, :, :], wgs_rows[:, 1:4, :])
+        for t in range(1, PACK):
+            nc.sync.dma_start(page[t][:], page_rows[:, t, :])
+        w4_codes = held([P, N], U32, "w4_codes")
+        nc.sync.dma_start(w4_codes[:].bitcast(I32), w4_words[0].rearrange("p n i -> p (n i)").bitcast(I32))
+        for q in range(4):
+            nc.sync.dma_start(w4_sc[32 * q : 32 * q + 4, :].bitcast(I32), w4_scales[0, 4 * q : 4 * q + 4, :].bitcast(I32))
+        nc.sync.dma_start(list3[:], offs3)
+        wg = [wg_first[:, 0, :]] + [wg_rest[:, t, :] for t in range(3)]
+
+        v_sc = held([P, S], U8, "v_sc")
+        nc.vector.tensor_copy(v_sc[:], tab_sc[:].indirect(list1[:]))
+        nc.gpsimd.dma_start(v_sc1[0:100, :].bitcast(I32), v_sc[4:104, :].bitcast(I32))
+        v = [held([P, S], U32, "v%d" % a) for a in range(2)]
+        for a in range(2):
+            nc.vector.tensor_copy(v[a][:], tab[a][:].indirect(list1[:]))
+
+        w2_codes = held([P, 2, 2 * H], U8, "w2_codes")
+        w2_sc = held([P, 2, H], U8, "w2_sc")
+        for a in range(2):
+            nc.vector.tensor_copy(
+                w2_codes[:, a, :].rearrange("p (t m b) -> p m t b", t=PACK, b=2),
+                w2_raw[:, a, :].rearrange("p (m t b) -> p m t b", t=PACK, b=2),
+            )
+        nc.vector.tensor_copy(
+            w2_sc[:].rearrange("p a (t m) -> p a m t", t=PACK),
+            w2_sc_raw[:].rearrange("p a (m t) -> p a m t", t=PACK),
+        )
+
+        def quantise_weight(raw, copy, name):
+            rounded = ring.tile([P, PACK * H], BF16, name="rounded", align_bytes=64)
+            copy(
+                rounded[:].rearrange("p (t m j) -> p m j t", t=PACK, j=PACK),
+                raw[:].rearrange("p j (m t) -> p m j t", t=PACK),
+            )
+            codes = held([P, H], U32, name + "_codes")
+            scales = held([P, H], U8, name + "_sc")
+            nc.vector.quantize_mx(out=codes[:].bitcast(FP8X4), scales=scales[:], in_=rounded[:])
+            return codes, scales
+
+        w1_q = [quantise_weight(w1_raw[a], (nc.scalar.copy, nc.vector.tensor_copy)[a], "w1_%d" % a) for a in range(2)]
+        w3_q = [quantise_weight(w3_raw[a], nc.vector.tensor_copy, "w3_%d" % a) for a in range(2)]
+
+        def product_fp8(acc, wq, t, h):
+            for a in range(2):
+                codes, scales = wq[a]
+                nc.tensor.matmul_mx(
+                    out=acc[:], lhsT=codes[:, cols(t, P)].bitcast(FP8X4), lhsT_scale=scales[:, cols(t, P)],
+                    rhs=v[a][:, cols(h, HALF)].bitcast(FP8X4), rhs_scale=v_sc[4 * a : P, cols(h, HALF)],
+                    start=(a == 0), stop=(a == 1),
+                )
+
+        def fold_gain(t):
+            nc.scalar.activation(wg[t], wg[t], ACT.Copy, scale=gain_sb[:, t : t + 1])
+
+        fold_gain(0)
+        units = [(t, h) for t in range(PACK) for h in range(2)]
+        work = {}
+        for t, h in units:
+            acc_b = psum.tile([P, HALF], F32, name="acc_b")
+            for a in range(2):
+                nc.tensor.matmul_mx(
+                    out=acc_b[:], lhsT=w2_codes[:, a, cols(t, 2 * P)].bitcast(FP4X4), lhsT_scale=w2_sc[:, a, cols(t, P)],
+                    rhs=v[a][:, cols(h, HALF)].bitcast(FP8X4), rhs_scale=(v_sc, v_sc1)[a][:, cols(h, HALF)],
+                    start=(a == 0), stop=(a == 1),
+                )
+            acc_a = psum.tile([P, HALF], F32, name="acc_a")
+            product_fp8(acc_a, w1_q, t, h)
+            u = held([P, HALF], F32, "u%d%d" % (t, h))
+            work[t, h] = u
+            nc.scalar.activation(u[:], acc_a[:], ACT.Tanh)
+            nc.vector.tensor_tensor(u[:], acc_b[:], u[:], ALU.add)
+            nc.scalar.activation(u[:], u[:], ACT.Abs)
+        for t in range(1, PACK):
+            fold_gain(t)
+
+        woven = held([P, T2, PACK], BF16, "woven")
+        out_rows = out_1.rearrange("(p t) m -> p t m", t=PACK)
+
+        def weave_page(t, c):
+            nc.scalar.copy(woven[:, cols(c, T2 // 2), t], page[t][:, cols(c, T2 // 2)])
+
+        for t in range(PACK):
+            for h in range(2):
+                acc_c = psum.tile([P, HALF], F32, name="acc_c")
+                product_fp8(acc_c, w3_q, t, h)
+                u = work[t, h]
+                nc.vector.tensor_tensor(u[:], acc_c[:], u[:], ALU.add)
+                nc.vector.tensor_tensor(page[t][:].indirect(list2[:, cols(h, LCOLS)]), u[:], wg[t][:, cols(h, HALF)], ALU.mult)
+            nc.sync.dma_start(out_rows[:, t, :], page[t][:])
+            if t < PACK - 1:
+                for c in range(2):
+                    weave_page(t, c)
+
+        for h in range(2):
+            weave_page(PACK - 1, h)
+            x_rows = ring.tile([P, PACK, HALF], BF16, name="x_rows", align_bytes=64)
+            for t in range(PACK):
+                picked = work[t, h]
+                nc.vector.tensor_copy(picked[:], page[t][:].indirect(list3[:, cols(h, LCOLS)]))
+                if t < PACK - 1:
+                    nc.scalar.activation(x_rows[:, t, :], picked[:], ACT.Identity, bias=bias_sb[:, t : t + 1])
+                else:
+                    nc.vector.tensor_scalar(x_rows[:, t, :], picked[:], bias_sb[:, t : t + 1], None, ALU.add)
+            x_woven = keep.tile([P, HALF * PACK], BF16, name="x_woven", tag="x_woven%d" % h, align_bytes=64)
+            nc.vector.tensor_copy(
+                x_woven[:].rearrange("p (c i t) -> p c t i", i=4, t=PACK),
+                x_rows[:].rearrange("p t (c i) -> p c t i", i=4),
+            )
+            x_codes = ring.tile([P, HALF], U32, name="x_codes", align_bytes=64)
+            x_sc = ring.tile([P, HALF], U8, name="x_sc", align_bytes=64)
+            nc.vector.quantize_mx(out=x_codes[:].bitcast(FP8X4), scales=x_sc[:], in_=x_woven[:])
+            for n in range(N // P):
+                acc_y = psum.tile([P, HALF], F32, name="acc_y")
+                nc.tensor.matmul_mx(
+                    out=acc_y[:], lhsT=w4_codes[:, cols(n, P)].bitcast(FP8X4), lhsT_scale=w4_sc[:, cols(n, P)],
+                    rhs=x_codes[:].bitcast(FP8X4), rhs_scale=x_sc[:], start=True, stop=True,
+                )
+                score = held([P, HALF], F32, "score%d%d" % (n, h))
+                nc.scalar.activation(score[:], acc_y[:], ACT.Square)
+                nc.sync.dma_start(out_0[cols(n, P), cols(h, HALF)], score[:])
+
+        y_codes = held([P, T2], U32, "y_codes")
+        y_sc = keep.tile([P, T2], U8, name="y_sc", tag="x_woven1", align_bytes=64)
+        for h in range(2):
+            c = cols(h, T2 // 2)
+            nc.vector.quantize_mx(
+                out=y_codes[:, c].bitcast(FP8X4), scales=y_sc[:, c], in_=woven[:, c, :].rearrange("p m t -> p (m t)")
+            )
+            nc.sync.dma_start(out_2[0, :, c, :].rearrange("p m i -> p (m i)").bitcast(I32), y_codes[:, c].bitcast(I32))
+        for q in range(4):
+            nc.sync.dma_start(out_3[0, 4 * q : 4 * q + 4, :].bitcast(I32), y_sc[32 * q : 32 * q + 4, :].bitcast(I32))

@@ -1,6 +1,7 @@
 from contextlib import ExitStack
 
 import concourse.mybir as mybir
+from concourse.masks import make_identity
 
 K, T, S, H, T2, NP, N = 1024, 4096, 1024, 512, 2048, 1024, 384
 FLOPS = 2 * (3 * K * H * S + H * N * NP)
@@ -20,6 +21,7 @@ P = 128
 PACK = 4
 HALF = 512
 LCOLS = HALF // 16
+BLOCKS = HALF // P
 
 
 def cols(i, width):
@@ -35,19 +37,20 @@ def tile_list_capsule_segment_scores_kernel(
         keep = ctx.enter_context(tc.tile_pool(name="keep", bufs=1))
         ring = ctx.enter_context(tc.tile_pool(name="ring", bufs=2))
         psum = ctx.enter_context(tc.psum_pool(name="psum", bufs=2))
+        psum_wide = ctx.enter_context(tc.psum_pool(name="psum_wide", bufs=4))
 
-        def held(shape, dtype, name):
-            return keep.tile(shape, dtype, name=name, align_bytes=64)
+        def held(shape, dtype, name, tag=None):
+            return keep.tile(shape, dtype, name=name, tag=tag or name, align_bytes=64)
 
         list1 = held([P, S // 16], U16, "list1")
         list2 = held([P, S // 16], U16, "list2")
         list3 = held([P, NP // 16], U16, "list3")
 
-        tab_sc = held([P, T], U8, "tab_sc")
-        w2_sc_raw = held([P, 2, H], U8, "w2_sc_raw")
-        v_sc1 = held([P, S], U8, "v_sc1")
+        tab_sc = held([P, 2, T], U8, "tab_sc")
+        w2_sc = held([P, 2, H], U8, "w2_sc")
         w4_sc = held([P, N], U8, "w4_sc")
-        for plane in (tab_sc[:], w2_sc_raw[:].rearrange("p a c -> p (a c)"), v_sc1[:], w4_sc[:]):
+        nc.gpsimd.memset(tab_sc[:, 0, :].bitcast(I32), 0)
+        for plane in (tab_sc[:, 1, :], w2_sc[:].rearrange("p a c -> p (a c)"), w4_sc[:]):
             nc.vector.memset(plane.bitcast(I32), 0)
 
         def load_weight(w, a, name):
@@ -55,37 +58,39 @@ def tile_list_capsule_segment_scores_kernel(
             nc.sync.dma_start(raw[:], w[512 * a : 512 * (a + 1), :].rearrange("(p j) c -> p j c", j=PACK))
             return raw
 
-        def load_table(a):
-            words = held([P, T], U32, "tab%d" % a)
-            nc.sync.dma_start(words[:].bitcast(I32), tab_words[a].rearrange("p t i -> p (t i)").bitcast(I32))
-            return words
+        tab = [held([P, T], U32, "tab%d" % a) for a in range(2)]
+
+        def load_table(a, part):
+            nc.sync.dma_start(tab[a][:, part].bitcast(I32), tab_words[a, :, part, :].rearrange("p t i -> p (t i)").bitcast(I32))
 
         nc.sync.dma_start(list1[:], offs)
-        tab = [load_table(0)]
+        load_table(0, cols(0, T // 2))
         for q in range(4):
-            nc.scalar.dma_start(tab_sc[32 * q : 32 * q + 8, :].bitcast(I32), tab_scales[:, 4 * q : 4 * q + 4, :].bitcast(I32))
-        w2_raw = held([P, 2, 2 * H], U8, "w2_raw")
-        nc.sync.dma_start(w2_raw[:].bitcast(I32), w2_words.rearrange("a p n -> p a n").bitcast(I32))
-        tab.append(load_table(1))
+            nc.sync.dma_start(
+                tab_sc[32 * q : 32 * q + 4, :, :].bitcast(I32),
+                tab_scales[:, 4 * q : 4 * q + 4, :].rearrange("a r c -> r a c").bitcast(I32),
+            )
+        load_table(0, cols(1, T // 2))
+        w2_codes = held([P, 2, 2 * H], U8, "w2_codes")
+        nc.sync.dma_start(w2_codes[:].bitcast(I32), w2_words.rearrange("a p n -> p a n").bitcast(I32))
         for q in range(4):
-            nc.scalar.dma_start(
-                w2_sc_raw[32 * q : 32 * q + 4, :, :].bitcast(I32),
+            nc.sync.dma_start(
+                w2_sc[32 * q : 32 * q + 4, :, :].bitcast(I32),
                 w2_scales[:, 4 * q : 4 * q + 4, :].rearrange("a r c -> r a c").bitcast(I32),
             )
+        gain_sb = held([P, PACK], F32, "gain_sb")
+        nc.sync.dma_start(gain_sb[:], gain.rearrange("(p t) -> p t", t=PACK))
+        nc.sync.dma_start(list2[:], offs2)
+        load_table(1, cols(0, T))
         w1_raw = [load_weight(w1, a, "w1_raw%d" % a) for a in range(2)]
         w3_raw = [load_weight(w3, a, "w3_raw%d" % a) for a in range(2)]
-        gain_sb = held([P, PACK], F32, "gain_sb")
-        nc.gpsimd.dma_start(gain_sb[:], gain.rearrange("(p t) -> p t", t=PACK))
-        bias_sb = held([P, PACK], F32, "bias_sb")
-        nc.gpsimd.dma_start(bias_sb[:], bias.rearrange("(p t) -> p t", t=PACK))
         wgs_rows = wgs.rearrange("(i t) j -> i t j", t=PACK)
         wg_first = held([P, 1, S], F32, "wg_first")
-        wg_rest = held([P, 3, S], F32, "wg_rest")
+        wg_rest = held([P, 3, S], F32, "wg_rest", tag="late")
         page_rows = page0.rearrange("(p t) m -> p t m", t=PACK)
         page = [held([P, T2], F32, "page%d" % t) for t in range(PACK)]
         for q in range(4):
             nc.sync.dma_start(wg_first[32 * q : 32 * q + 32, :, :], wgs_rows[:, 0:1, :])
-        nc.sync.dma_start(list2[:], offs2)
         nc.sync.dma_start(page[0][:], page_rows[:, 0, :])
         for q in range(4):
             nc.sync.dma_start(wg_rest[32 * q : 32 * q + 32, :, :], wgs_rows[:, 1:4, :])
@@ -95,123 +100,165 @@ def tile_list_capsule_segment_scores_kernel(
         nc.sync.dma_start(w4_codes[:].bitcast(I32), w4_words[0].rearrange("p n i -> p (n i)").bitcast(I32))
         for q in range(4):
             nc.sync.dma_start(w4_sc[32 * q : 32 * q + 4, :].bitcast(I32), w4_scales[0, 4 * q : 4 * q + 4, :].bitcast(I32))
+        bias_sb = held([P, PACK], F32, "bias_sb")
+        nc.sync.dma_start(bias_sb[:], bias.rearrange("(p t) -> p t", t=PACK))
         nc.sync.dma_start(list3[:], offs3)
         wg = [wg_first[:, 0, :]] + [wg_rest[:, t, :] for t in range(3)]
 
-        v_sc = held([P, S], U8, "v_sc")
-        nc.vector.tensor_copy(v_sc[:], tab_sc[:].indirect(list1[:]))
-        nc.gpsimd.dma_start(v_sc1[0:100, :].bitcast(I32), v_sc[4:104, :].bitcast(I32))
-        v = [held([P, S], U32, "v%d" % a) for a in range(2)]
+        ident = held([P, P], F32, "ident")
+        make_identity(nc, ident[:])
+        v = [[held([P, HALF], U32, "v%d%d" % (a, h)) for h in range(2)] for a in range(2)]
+        v_sc = [held([P, S], U8, "v_sc%d" % a) for a in range(2)]
         for a in range(2):
-            nc.vector.tensor_copy(v[a][:], tab[a][:].indirect(list1[:]))
-
-        w2_codes = held([P, 2, 2 * H], U8, "w2_codes")
-        w2_sc = held([P, 2, H], U8, "w2_sc")
+            nc.vector.tensor_copy(v_sc[a][:], tab_sc[:, a, :].indirect(list1[:]))
         for a in range(2):
-            nc.vector.tensor_copy(
-                w2_codes[:, a, :].rearrange("p (t m b) -> p m t b", t=PACK, b=2),
-                w2_raw[:, a, :].rearrange("p (m t b) -> p m t b", t=PACK, b=2),
-            )
-        nc.vector.tensor_copy(
-            w2_sc[:].rearrange("p a (t m) -> p a m t", t=PACK),
-            w2_sc_raw[:].rearrange("p a (m t) -> p a m t", t=PACK),
-        )
+            for h in range(2):
+                nc.vector.tensor_copy(v[a][h][:], tab[a][:].indirect(list1[:, cols(h, LCOLS)]))
 
-        def quantise_weight(raw, copy, name):
-            rounded = ring.tile([P, PACK * H], BF16, name="rounded", align_bytes=64)
-            copy(
-                rounded[:].rearrange("p (t m j) -> p m j t", t=PACK, j=PACK),
-                raw[:].rearrange("p j (m t) -> p m j t", t=PACK),
-            )
+        def quantise(rounded, name):
             codes = held([P, H], U32, name + "_codes")
             scales = held([P, H], U8, name + "_sc")
             nc.vector.quantize_mx(out=codes[:].bitcast(FP8X4), scales=scales[:], in_=rounded[:])
             return codes, scales
 
-        w1_q = [quantise_weight(w1_raw[a], (nc.scalar.copy, nc.vector.tensor_copy)[a], "w1_%d" % a) for a in range(2)]
-        w3_q = [quantise_weight(w3_raw[a], nc.vector.tensor_copy, "w3_%d" % a) for a in range(2)]
+        w1_q, w3_q = [], []
+        for a in range(2):
+            rounded = ring.tile([P, PACK * H], BF16, name="rounded", align_bytes=64)
+            nc.vector.tensor_copy(
+                rounded[:].rearrange("p (c i j) -> p c j i", i=4, j=PACK),
+                w1_raw[a][:].rearrange("p j (c i) -> p c j i", i=4),
+            )
+            w1_q.append(quantise(rounded, "w1_%d" % a))
+        for a in range(2):
+            rounded = ring.tile([P, PACK * H], BF16, name="rounded", align_bytes=64)
+            nc.vector.tensor_copy(
+                rounded[:].rearrange("p (t m j) -> p m j t", t=PACK, j=PACK),
+                w3_raw[a][:].rearrange("p j (m t) -> p m j t", t=PACK),
+            )
+            w3_q.append(quantise(rounded, "w3_%d" % a))
 
-        def product_fp8(acc, wq, t, h):
-            for a in range(2):
-                codes, scales = wq[a]
-                nc.tensor.matmul_mx(
-                    out=acc[:], lhsT=codes[:, cols(t, P)].bitcast(FP8X4), lhsT_scale=scales[:, cols(t, P)],
-                    rhs=v[a][:, cols(h, HALF)].bitcast(FP8X4), rhs_scale=v_sc[4 * a : P, cols(h, HALF)],
-                    start=(a == 0), stop=(a == 1),
-                )
+        def dealt(acc):
+            return acc[:].rearrange("p (m t) -> p t m", t=PACK)
 
-        def fold_gain(t):
-            nc.scalar.activation(wg[t], wg[t], ACT.Copy, scale=gain_sb[:, t : t + 1])
+        b_turned = held([P, 2 * BLOCKS, PACK, P], F32, "b_turned", tag="tab0")
+        for h in range(2):
+            for i in range(BLOCKS):
+                acc = psum_wide.tile([P, H], F32, name="acc")
+                for a in range(2):
+                    nc.tensor.matmul_mx(
+                        out=acc[:], lhsT=v[a][h][:, cols(i, P)].bitcast(FP8X4),
+                        lhsT_scale=v_sc[a][:, cols(BLOCKS * h + i, P)],
+                        rhs=w2_codes[:, a, :].bitcast(FP4X4), rhs_scale=w2_sc[:, a, :],
+                        start=(a == 0), stop=(a == 1),
+                    )
+                nc.scalar.copy(b_turned[:, BLOCKS * h + i, :, :], dealt(acc))
 
-        fold_gain(0)
-        units = [(t, h) for t in range(PACK) for h in range(2)]
+        def first_product(h):
+            a_turned = held([P, BLOCKS, PACK, P], F32, "a_turned%d" % h, tag="w1_raw%d" % h)
+            for i in range(BLOCKS):
+                acc = psum_wide.tile([P, H], F32, name="acc")
+                for a in range(2):
+                    codes, scales = w1_q[a]
+                    nc.tensor.matmul_mx(
+                        out=acc[:], lhsT=v[a][h][:, cols(i, P)].bitcast(FP8X4),
+                        lhsT_scale=v_sc[a][:, cols(BLOCKS * h + i, P)],
+                        rhs=codes[:].bitcast(FP8X4), rhs_scale=scales[:],
+                        start=(a == 0), stop=(a == 1),
+                    )
+                nc.scalar.activation(a_turned[:, i, :, :], dealt(acc), ACT.Tanh)
+            return a_turned
+
         work = {}
-        for t, h in units:
-            acc_b = psum.tile([P, HALF], F32, name="acc_b")
-            for a in range(2):
-                nc.tensor.matmul_mx(
-                    out=acc_b[:], lhsT=w2_codes[:, a, cols(t, 2 * P)].bitcast(FP4X4), lhsT_scale=w2_sc[:, a, cols(t, P)],
-                    rhs=v[a][:, cols(h, HALF)].bitcast(FP8X4), rhs_scale=(v_sc, v_sc1)[a][:, cols(h, HALF)],
-                    start=(a == 0), stop=(a == 1),
-                )
-            acc_a = psum.tile([P, HALF], F32, name="acc_a")
-            product_fp8(acc_a, w1_q, t, h)
-            u = held([P, HALF], F32, "u%d%d" % (t, h))
-            work[t, h] = u
-            nc.scalar.activation(u[:], acc_a[:], ACT.Tanh)
-            nc.vector.tensor_tensor(u[:], acc_b[:], u[:], ALU.add)
-            nc.scalar.activation(u[:], u[:], ACT.Abs)
-        for t in range(1, PACK):
-            fold_gain(t)
 
-        woven = held([P, T2, PACK], BF16, "woven")
+        def sum_and_abs(a_turned, t, h):
+            acc_u = psum.tile([P, HALF], F32, name="acc_u")
+            terms = [b_turned[:, BLOCKS * h + i, t, :] for i in range(BLOCKS)] + [a_turned[:, i, t, :] for i in range(BLOCKS)]
+            for n, term in enumerate(terms):
+                nc.tensor.matmul(
+                    acc_u[:, cols(n % BLOCKS, P)], lhsT=term, rhs=ident[:],
+                    start=(n == 0), stop=(n == len(terms) - 1), is_transpose=True,
+                )
+            work[t, h] = held([P, HALF], F32, "b%d%d" % (t, h))
+            nc.scalar.activation(work[t, h][:], acc_u[:], ACT.Abs)
+
+        factor = held([P, PACK, S], F32, "factor", tag="tab1")
+
+        def fold_gain(t, h):
+            nc.scalar.activation(factor[:, t, cols(h, HALF)], wg[t][:, cols(h, HALF)], ACT.Copy, scale=gain_sb[:, t : t + 1])
+
         out_rows = out_1.rearrange("(p t) m -> p t m", t=PACK)
 
-        def weave_page(t, c):
-            nc.scalar.copy(woven[:, cols(c, T2 // 2), t], page[t][:, cols(c, T2 // 2)])
+        def weave_page(t, c, parts):
+            nc.scalar.copy(woven[:, cols(c, T2 // parts), t], page[t][:, cols(c, T2 // parts)])
 
-        for t in range(PACK):
+        def put(t, h):
+            acc_c = psum.tile([P, HALF], F32, name="acc_c")
+            for a in range(2):
+                codes, scales = w3_q[a]
+                nc.tensor.matmul_mx(
+                    out=acc_c[:], lhsT=codes[:, cols(t, P)].bitcast(FP8X4), lhsT_scale=scales[:, cols(t, P)],
+                    rhs=v[a][h][:].bitcast(FP8X4), rhs_scale=v_sc[a][:, cols(h, HALF)],
+                    start=(a == 0), stop=(a == 1),
+                )
+            summed = ring.tile([P, HALF], F32, name="summed", align_bytes=64)
+            nc.vector.tensor_tensor(summed[:], acc_c[:], work[t, h][:], ALU.add)
+            nc.vector.tensor_tensor(page[t][:].indirect(list2[:, cols(h, LCOLS)]), summed[:], factor[:, t, cols(h, HALF)], ALU.mult)
+
+        a_halves = []
+        for h in range(2):
+            a_halves.append(first_product(h))
+            sum_and_abs(a_halves[h], 0, h)
+            fold_gain(0, h)
+            put(0, h)
+        for t in range(1, PACK):
             for h in range(2):
-                acc_c = psum.tile([P, HALF], F32, name="acc_c")
-                product_fp8(acc_c, w3_q, t, h)
-                u = work[t, h]
-                nc.vector.tensor_tensor(u[:], acc_c[:], u[:], ALU.add)
-                nc.vector.tensor_tensor(page[t][:].indirect(list2[:, cols(h, LCOLS)]), u[:], wg[t][:, cols(h, HALF)], ALU.mult)
+                sum_and_abs(a_halves[h], t, h)
+                fold_gain(t, h)
+        woven = held([P, T2, PACK], BF16, "woven", tag="late")
+        for t in range(PACK):
+            if t > 0:
+                for h in range(2):
+                    put(t, h)
             nc.sync.dma_start(out_rows[:, t, :], page[t][:])
             if t < PACK - 1:
                 for c in range(2):
-                    weave_page(t, c)
+                    weave_page(t, c, 2)
 
+        picked_all = held([P, 2, PACK, HALF], F32, "picked_all", tag="tab1")
+        weave_page(PACK - 1, 0, 4)
         for h in range(2):
-            weave_page(PACK - 1, h)
             x_rows = ring.tile([P, PACK, HALF], BF16, name="x_rows", align_bytes=64)
             for t in range(PACK):
-                picked = work[t, h]
-                nc.vector.tensor_copy(picked[:], page[t][:].indirect(list3[:, cols(h, LCOLS)]))
-                if t < PACK - 1:
-                    nc.scalar.activation(x_rows[:, t, :], picked[:], ACT.Identity, bias=bias_sb[:, t : t + 1])
+                picked = picked_all[:, h, t, :]
+                nc.vector.tensor_copy(picked, page[t][:].indirect(list3[:, cols(h, LCOLS)]))
+                if h == 0:
+                    nc.scalar.activation(x_rows[:, t, :], picked, ACT.Identity, bias=bias_sb[:, t : t + 1])
                 else:
-                    nc.vector.tensor_scalar(x_rows[:, t, :], picked[:], bias_sb[:, t : t + 1], None, ALU.add)
-            x_woven = keep.tile([P, HALF * PACK], BF16, name="x_woven", tag="x_woven%d" % h, align_bytes=64)
-            nc.vector.tensor_copy(
+                    nc.vector.tensor_scalar(x_rows[:, t, :], picked, bias_sb[:, t : t + 1], None, ALU.add)
+            if h == 0:
+                weave_page(PACK - 1, 1, 4)
+            x_woven = held([P, HALF * PACK], BF16, "x_woven", tag="x_woven")
+            (nc.scalar.copy, nc.vector.tensor_copy)[h](
                 x_woven[:].rearrange("p (c i t) -> p c t i", i=4, t=PACK),
                 x_rows[:].rearrange("p t (c i) -> p c t i", i=4),
             )
+            if h == 0:
+                weave_page(PACK - 1, 1, 2)
             x_codes = ring.tile([P, HALF], U32, name="x_codes", align_bytes=64)
             x_sc = ring.tile([P, HALF], U8, name="x_sc", align_bytes=64)
             nc.vector.quantize_mx(out=x_codes[:].bitcast(FP8X4), scales=x_sc[:], in_=x_woven[:])
             for n in range(N // P):
-                acc_y = psum.tile([P, HALF], F32, name="acc_y")
+                acc = psum_wide.tile([P, HALF], F32, name="acc")
                 nc.tensor.matmul_mx(
-                    out=acc_y[:], lhsT=w4_codes[:, cols(n, P)].bitcast(FP8X4), lhsT_scale=w4_sc[:, cols(n, P)],
+                    out=acc[:], lhsT=w4_codes[:, cols(n, P)].bitcast(FP8X4), lhsT_scale=w4_sc[:, cols(n, P)],
                     rhs=x_codes[:].bitcast(FP8X4), rhs_scale=x_sc[:], start=True, stop=True,
                 )
                 score = held([P, HALF], F32, "score%d%d" % (n, h))
-                nc.scalar.activation(score[:], acc_y[:], ACT.Square)
+                nc.scalar.activation(score[:], acc[:], ACT.Square)
                 nc.sync.dma_start(out_0[cols(n, P), cols(h, HALF)], score[:])
 
         y_codes = held([P, T2], U32, "y_codes")
-        y_sc = keep.tile([P, T2], U8, name="y_sc", tag="x_woven1", align_bytes=64)
+        y_sc = held([P, T2], U8, "y_sc", tag="x_woven")
         for h in range(2):
             c = cols(h, T2 // 2)
             nc.vector.quantize_mx(

from contextlib import ExitStack

import concourse.mybir as mybir
from concourse.masks import make_identity

K, T, S, H, T2, NP, N = 1024, 4096, 1024, 512, 2048, 1024, 384
FLOPS = 2 * (3 * K * H * S + H * N * NP)

F32 = mybir.dt.float32
BF16 = mybir.dt.bfloat16
I32 = mybir.dt.int32
U32 = mybir.dt.uint32
U16 = mybir.dt.uint16
U8 = mybir.dt.uint8
FP8X4 = mybir.dt.float8_e4m3fn_x4
FP4X4 = mybir.dt.float4_e2m1fn_x4
ACT = mybir.ActivationFunctionType
ALU = mybir.AluOpType

P = 128
PACK = 4
HALF = 512
LCOLS = HALF // 16
BLOCKS = HALF // P


def cols(i, width):
    return slice(i * width, (i + 1) * width)


def tile_list_capsule_segment_scores_kernel(
    tc, tab_words, tab_scales, offs, offs2, offs3, w1, w2_words, w2_scales, w3, gain, wgs, page0, bias,
    w4_words, w4_scales, out_0, out_1, out_2, out_3,
):
    nc = tc.nc
    with ExitStack() as ctx:
        keep = ctx.enter_context(tc.tile_pool(name="keep", bufs=1))
        ring = ctx.enter_context(tc.tile_pool(name="ring", bufs=2))
        psum = ctx.enter_context(tc.psum_pool(name="psum", bufs=2))
        psum_wide = ctx.enter_context(tc.psum_pool(name="psum_wide", bufs=4))

        def held(shape, dtype, name, tag=None):
            return keep.tile(shape, dtype, name=name, tag=tag or name, align_bytes=64)

        list1 = held([P, S // 16], U16, "list1")
        list2 = held([P, S // 16], U16, "list2")
        list3 = held([P, NP // 16], U16, "list3")

        tab_sc = held([P, 2, T], U8, "tab_sc")
        w2_sc = held([P, 2, H], U8, "w2_sc")
        w4_sc = held([P, N], U8, "w4_sc")
        nc.gpsimd.memset(tab_sc[:, 0, :].bitcast(I32), 0)
        for plane in (tab_sc[:, 1, :], w2_sc[:].rearrange("p a c -> p (a c)"), w4_sc[:]):
            nc.vector.memset(plane.bitcast(I32), 0)

        def load_weight(w, a, name):
            raw = held([P, PACK, H], F32, name)
            nc.sync.dma_start(raw[:], w[512 * a : 512 * (a + 1), :].rearrange("(p j) c -> p j c", j=PACK))
            return raw

        tab = [held([P, T], U32, "tab%d" % a) for a in range(2)]

        def load_table(a, part):
            nc.sync.dma_start(tab[a][:, part].bitcast(I32), tab_words[a, :, part, :].rearrange("p t i -> p (t i)").bitcast(I32))

        nc.sync.dma_start(list1[:], offs)
        load_table(0, cols(0, T // 2))
        for q in range(4):
            nc.sync.dma_start(
                tab_sc[32 * q : 32 * q + 4, :, :].bitcast(I32),
                tab_scales[:, 4 * q : 4 * q + 4, :].rearrange("a r c -> r a c").bitcast(I32),
            )
        load_table(0, cols(1, T // 2))
        w2_codes = held([P, 2, 2 * H], U8, "w2_codes")
        nc.sync.dma_start(w2_codes[:].bitcast(I32), w2_words.rearrange("a p n -> p a n").bitcast(I32))
        for q in range(4):
            nc.sync.dma_start(
                w2_sc[32 * q : 32 * q + 4, :, :].bitcast(I32),
                w2_scales[:, 4 * q : 4 * q + 4, :].rearrange("a r c -> r a c").bitcast(I32),
            )
        gain_sb = held([P, PACK], F32, "gain_sb")
        nc.sync.dma_start(gain_sb[:], gain.rearrange("(p t) -> p t", t=PACK))
        nc.sync.dma_start(list2[:], offs2)
        load_table(1, cols(0, T))
        w1_raw = [load_weight(w1, a, "w1_raw%d" % a) for a in range(2)]
        w3_raw = [load_weight(w3, a, "w3_raw%d" % a) for a in range(2)]
        wgs_rows = wgs.rearrange("(i t) j -> i t j", t=PACK)
        wg_first = held([P, 1, S], F32, "wg_first")
        wg_rest = held([P, 3, S], F32, "wg_rest", tag="late")
        page_rows = page0.rearrange("(p t) m -> p t m", t=PACK)
        page = [held([P, T2], F32, "page%d" % t) for t in range(PACK)]
        for q in range(4):
            nc.sync.dma_start(wg_first[32 * q : 32 * q + 32, :, :], wgs_rows[:, 0:1, :])
        nc.sync.dma_start(page[0][:], page_rows[:, 0, :])
        for q in range(4):
            nc.sync.dma_start(wg_rest[32 * q : 32 * q + 32, :, :], wgs_rows[:, 1:4, :])
        for t in range(1, PACK):
            nc.sync.dma_start(page[t][:], page_rows[:, t, :])
        w4_codes = held([P, N], U32, "w4_codes")
        nc.sync.dma_start(w4_codes[:].bitcast(I32), w4_words[0].rearrange("p n i -> p (n i)").bitcast(I32))
        for q in range(4):
            nc.sync.dma_start(w4_sc[32 * q : 32 * q + 4, :].bitcast(I32), w4_scales[0, 4 * q : 4 * q + 4, :].bitcast(I32))
        bias_sb = held([P, PACK], F32, "bias_sb")
        nc.sync.dma_start(bias_sb[:], bias.rearrange("(p t) -> p t", t=PACK))
        nc.sync.dma_start(list3[:], offs3)
        wg = [wg_first[:, 0, :]] + [wg_rest[:, t, :] for t in range(3)]

        ident = held([P, P], F32, "ident")
        make_identity(nc, ident[:])
        v = [[held([P, HALF], U32, "v%d%d" % (a, h)) for h in range(2)] for a in range(2)]
        v_sc = [held([P, S], U8, "v_sc%d" % a) for a in range(2)]
        for a in range(2):
            nc.vector.tensor_copy(v_sc[a][:], tab_sc[:, a, :].indirect(list1[:]))
        for a in range(2):
            for h in range(2):
                nc.vector.tensor_copy(v[a][h][:], tab[a][:].indirect(list1[:, cols(h, LCOLS)]))

        def quantise(rounded, name):
            codes = held([P, H], U32, name + "_codes")
            scales = held([P, H], U8, name + "_sc")
            nc.vector.quantize_mx(out=codes[:].bitcast(FP8X4), scales=scales[:], in_=rounded[:])
            return codes, scales

        w1_q, w3_q = [], []
        for a in range(2):
            rounded = ring.tile([P, PACK * H], BF16, name="rounded", align_bytes=64)
            nc.vector.tensor_copy(
                rounded[:].rearrange("p (c i j) -> p c j i", i=4, j=PACK),
                w1_raw[a][:].rearrange("p j (c i) -> p c j i", i=4),
            )
            w1_q.append(quantise(rounded, "w1_%d" % a))
        for a in range(2):
            rounded = ring.tile([P, PACK * H], BF16, name="rounded", align_bytes=64)
            nc.vector.tensor_copy(
                rounded[:].rearrange("p (t m j) -> p m j t", t=PACK, j=PACK),
                w3_raw[a][:].rearrange("p j (m t) -> p m j t", t=PACK),
            )
            w3_q.append(quantise(rounded, "w3_%d" % a))

        def dealt(acc):
            return acc[:].rearrange("p (m t) -> p t m", t=PACK)

        b_turned = held([P, 2 * BLOCKS, PACK, P], F32, "b_turned", tag="tab0")
        for h in range(2):
            for i in range(BLOCKS):
                acc = psum_wide.tile([P, H], F32, name="acc")
                for a in range(2):
                    nc.tensor.matmul_mx(
                        out=acc[:], lhsT=v[a][h][:, cols(i, P)].bitcast(FP8X4),
                        lhsT_scale=v_sc[a][:, cols(BLOCKS * h + i, P)],
                        rhs=w2_codes[:, a, :].bitcast(FP4X4), rhs_scale=w2_sc[:, a, :],
                        start=(a == 0), stop=(a == 1),
                    )
                nc.scalar.copy(b_turned[:, BLOCKS * h + i, :, :], dealt(acc))

        def first_product(h):
            a_turned = held([P, BLOCKS, PACK, P], F32, "a_turned%d" % h, tag="w1_raw%d" % h)
            for i in range(BLOCKS):
                acc = psum_wide.tile([P, H], F32, name="acc")
                for a in range(2):
                    codes, scales = w1_q[a]
                    nc.tensor.matmul_mx(
                        out=acc[:], lhsT=v[a][h][:, cols(i, P)].bitcast(FP8X4),
                        lhsT_scale=v_sc[a][:, cols(BLOCKS * h + i, P)],
                        rhs=codes[:].bitcast(FP8X4), rhs_scale=scales[:],
                        start=(a == 0), stop=(a == 1),
                    )
                nc.scalar.activation(a_turned[:, i, :, :], dealt(acc), ACT.Tanh)
            return a_turned

        work = {}

        def sum_and_abs(a_turned, t, h):
            acc_u = psum.tile([P, HALF], F32, name="acc_u")
            terms = [b_turned[:, BLOCKS * h + i, t, :] for i in range(BLOCKS)] + [a_turned[:, i, t, :] for i in range(BLOCKS)]
            for n, term in enumerate(terms):
                nc.tensor.matmul(
                    acc_u[:, cols(n % BLOCKS, P)], lhsT=term, rhs=ident[:],
                    start=(n == 0), stop=(n == len(terms) - 1), is_transpose=True,
                )
            work[t, h] = held([P, HALF], F32, "b%d%d" % (t, h))
            nc.scalar.activation(work[t, h][:], acc_u[:], ACT.Abs)

        factor = held([P, PACK, S], F32, "factor", tag="tab1")

        def fold_gain(t, h):
            nc.scalar.activation(factor[:, t, cols(h, HALF)], wg[t][:, cols(h, HALF)], ACT.Copy, scale=gain_sb[:, t : t + 1])

        out_rows = out_1.rearrange("(p t) m -> p t m", t=PACK)

        def weave_page(t, c, parts):
            nc.scalar.copy(woven[:, cols(c, T2 // parts), t], page[t][:, cols(c, T2 // parts)])

        def put(t, h):
            acc_c = psum.tile([P, HALF], F32, name="acc_c")
            for a in range(2):
                codes, scales = w3_q[a]
                nc.tensor.matmul_mx(
                    out=acc_c[:], lhsT=codes[:, cols(t, P)].bitcast(FP8X4), lhsT_scale=scales[:, cols(t, P)],
                    rhs=v[a][h][:].bitcast(FP8X4), rhs_scale=v_sc[a][:, cols(h, HALF)],
                    start=(a == 0), stop=(a == 1),
                )
            summed = ring.tile([P, HALF], F32, name="summed", align_bytes=64)
            nc.vector.tensor_tensor(summed[:], acc_c[:], work[t, h][:], ALU.add)
            nc.vector.tensor_tensor(page[t][:].indirect(list2[:, cols(h, LCOLS)]), summed[:], factor[:, t, cols(h, HALF)], ALU.mult)

        a_halves = []
        for h in range(2):
            a_halves.append(first_product(h))
            sum_and_abs(a_halves[h], 0, h)
            fold_gain(0, h)
            put(0, h)
        for t in range(1, PACK):
            for h in range(2):
                sum_and_abs(a_halves[h], t, h)
                fold_gain(t, h)
        woven = held([P, T2, PACK], BF16, "woven", tag="late")
        for t in range(PACK):
            if t > 0:
                for h in range(2):
                    put(t, h)
            nc.sync.dma_start(out_rows[:, t, :], page[t][:])
            if t < PACK - 1:
                for c in range(2):
                    weave_page(t, c, 2)

        picked_all = held([P, 2, PACK, HALF], F32, "picked_all", tag="tab1")
        weave_page(PACK - 1, 0, 4)
        for h in range(2):
            x_rows = ring.tile([P, PACK, HALF], BF16, name="x_rows", align_bytes=64)
            for t in range(PACK):
                picked = picked_all[:, h, t, :]
                nc.vector.tensor_copy(picked, page[t][:].indirect(list3[:, cols(h, LCOLS)]))
                if h == 0:
                    nc.scalar.activation(x_rows[:, t, :], picked, ACT.Identity, bias=bias_sb[:, t : t + 1])
                else:
                    nc.vector.tensor_scalar(x_rows[:, t, :], picked, bias_sb[:, t : t + 1], None, ALU.add)
            if h == 0:
                weave_page(PACK - 1, 1, 4)
            x_woven = held([P, HALF * PACK], BF16, "x_woven", tag="x_woven")
            (nc.scalar.copy, nc.vector.tensor_copy)[h](
                x_woven[:].rearrange("p (c i t) -> p c t i", i=4, t=PACK),
                x_rows[:].rearrange("p t (c i) -> p c t i", i=4),
            )
            if h == 0:
                weave_page(PACK - 1, 1, 2)
            x_codes = ring.tile([P, HALF], U32, name="x_codes", align_bytes=64)
            x_sc = ring.tile([P, HALF], U8, name="x_sc", align_bytes=64)
            nc.vector.quantize_mx(out=x_codes[:].bitcast(FP8X4), scales=x_sc[:], in_=x_woven[:])
            for n in range(N // P):
                acc = psum_wide.tile([P, HALF], F32, name="acc")
                nc.tensor.matmul_mx(
                    out=acc[:], lhsT=w4_codes[:, cols(n, P)].bitcast(FP8X4), lhsT_scale=w4_sc[:, cols(n, P)],
                    rhs=x_codes[:].bitcast(FP8X4), rhs_scale=x_sc[:], start=True, stop=True,
                )
                score = held([P, HALF], F32, "score%d%d" % (n, h))
                nc.scalar.activation(score[:], acc[:], ACT.Square)
                nc.sync.dma_start(out_0[cols(n, P), cols(h, HALF)], score[:])

        y_codes = held([P, T2], U32, "y_codes")
        y_sc = held([P, T2], U8, "y_sc", tag="x_woven")
        for h in range(2):
            c = cols(h, T2 // 2)
            nc.vector.quantize_mx(
                out=y_codes[:, c].bitcast(FP8X4), scales=y_sc[:, c], in_=woven[:, c, :].rearrange("p m t -> p (m t)")
            )
            nc.sync.dma_start(out_2[0, :, c, :].rearrange("p m i -> p (m i)").bitcast(I32), y_codes[:, c].bitcast(I32))
        for q in range(4):
            nc.sync.dma_start(out_3[0, 4 * q : 4 * q + 4, :].bitcast(I32), y_sc[32 * q : 32 * q + 4, :].bitcast(I32))
